import numpy as np
import ml_dtypes


def mxq(x, axis, fmt="e4m3"):
    dtype, down = {"e4m3": (ml_dtypes.float8_e4m3fn, 7), "e5m2": (ml_dtypes.float8_e5m2, 14)}[fmt]
    v = np.moveaxis(np.asarray(x, np.float32).astype(ml_dtypes.bfloat16).astype(np.float64), axis, -1)
    blocks = v.reshape(v.shape[:-1] + (-1, 32))
    amax = np.abs(blocks).max(-1, keepdims=True)
    byte = np.maximum(np.where(amax > 0, np.frexp(amax)[1] - 1 + 127, 0) - down, 1)
    scale = np.exp2(byte - 127.0)
    codes = (blocks / scale).astype(np.float32).astype(dtype).astype(np.float64)
    return np.moveaxis((codes * scale).reshape(v.shape), -1, axis)


WIDE = False


def mx_kscale(k):
    if not WIDE:
        return np.ones(k)
    levels = np.array([10, -10, 5, -5, 0])
    if k % 512:
        return np.exp2(np.random.permutation(np.resize(levels, k // 32))).repeat(32)
    a = np.empty((k // 512, 16))
    for p in range(k // 512):
        a[p, :8] = np.random.permutation(np.resize(levels, 8))
        for g in range(8):
            far = levels[np.abs(levels - a[p, g]) >= 10]
            a[p, g + 8] = far[np.random.randint(len(far))]
    return np.exp2(a.ravel()).repeat(32)


def f64(x):
    return np.asarray(x).astype(np.float64)


def striped8(idx):
    return np.concatenate([x.reshape(-1, 16).T for x in idx]).astype(np.uint16)


def runs(offs, k):
    lists = np.stack([offs[16 * r : 16 * r + 16].T.reshape(-1) for r in range(8)]).astype(np.int64)
    return lists[np.arange(k) % 512 // 64]


def pack_weight(w):
    k, n = w.shape
    w = f64(np.asarray(w, np.float32).astype(ml_dtypes.bfloat16)).reshape(k // 32, 32, n)
    amax = np.abs(w).max(1)
    byte = np.clip(np.where(amax > 0, np.frexp(amax)[1] - 1 + 127 - 7, 1), 1, 254)
    scaled = (w * np.exp2(127.0 - byte)[:, None, :]).reshape(k, n).astype(np.float32)
    words = np.ascontiguousarray(scaled.reshape(k // 512, 128, 4, n).transpose(0, 1, 3, 2)).astype(ml_dtypes.float8_e4m3fn).view(np.uint8)
    return words, np.ascontiguousarray(byte.astype(np.uint8).reshape(k // 512, 16, n))


def unpack_weight(words, scales):
    g, p, n, _ = words.shape
    vals = np.ascontiguousarray(words).view(ml_dtypes.float8_e4m3fn).astype(np.float64) * np.repeat(np.exp2(scales.astype(np.float64) - 127.0), 8, axis=1)[..., None]
    return vals.transpose(0, 1, 3, 2).reshape(g * 512, n)


E2M1 = np.array([0.0, 0.5, 1.0, 1.5, 2.0, 3.0, 4.0, 6.0, -0.0, -0.5, -1.0, -1.5, -2.0, -3.0, -4.0, -6.0])


def pack_fp4(w):
    k, n = w.shape
    w = f64(np.asarray(w, np.float32).astype(ml_dtypes.bfloat16)).reshape(k // 32, 32, n)
    amax = np.abs(w).max(1)
    mant, ex = np.frexp(amax / 6.0)
    byte = np.clip(np.where(amax > 0, np.where(mant > 0.5, ex, ex - 1) + 127, 1), 1, 254)
    scaled = (w * np.exp2(127.0 - byte)[:, None, :]).reshape(k, n).astype(np.float32)
    c = np.ascontiguousarray(scaled.reshape(k // 512, 128, 4, n).transpose(0, 1, 3, 2)).astype(ml_dtypes.float4_e2m1fn).view(np.uint8) & 0xF
    words = (c[..., 0::2] | (c[..., 1::2] << 4)).reshape(k // 512, 128, 2 * n)
    return np.ascontiguousarray(words), np.ascontiguousarray(byte.astype(np.uint8).reshape(k // 512, 16, n))


def unpack_fp4(words, scales):
    g, _, n = scales.shape
    words = np.ascontiguousarray(words).reshape(g, 128, n, 2)
    nib = np.empty((g, 128, n, 4), np.uint8)
    nib[..., 0::2] = words & 0xF
    nib[..., 1::2] = words >> 4
    vals = E2M1[nib] * np.repeat(np.exp2(scales.astype(np.float64) - 127.0), 8, axis=1)[..., None]
    return vals.transpose(0, 1, 3, 2).reshape(g * 512, n)


K, T, S, H, G, U = 512, 1024, 512, 512, 2048, 1024


def setup_inputs():
    n = np.random.standard_normal
    s = mx_kscale(K)[:, None]
    packed_xT = pack_weight(n((K, T)) * s)
    packed_w1 = pack_fp4(n((K, H)) / np.sqrt(2 * K) / s)
    packed_w2 = pack_fp4(n((K, H)) / np.sqrt(2 * K) / s)
    packed_dT = pack_weight(n((K, G)) / s)
    return {
        "x_words": packed_xT[0],
        "x_scales": packed_xT[1],
        "w1_words": packed_w1[0],
        "w1_scales": packed_w1[1],
        "w2_words": packed_w2[0],
        "w2_scales": packed_w2[1],
        "gs": (np.random.uniform(0.5, 1.5, (K, 1)) * s).astype(np.float32),
        "d_words": packed_dT[0],
        "d_scales": packed_dT[1],
        "mem": n((H, U)).astype(np.float32),
        "offs": striped8(np.random.randint(0, T, (8, S))),
        "hz": striped8(np.random.randint(0, T, (8, S))),
        "n1": striped8(np.stack([np.random.permutation(S) for _ in range(8)])),
        "n2": striped8(np.stack([np.random.permutation(S) for _ in range(8)])),
        "k1": striped8(np.random.randint(0, G, (8, H))),
        "n3": striped8(np.stack([np.random.permutation(U)[:S] for _ in range(8)])),
    }


def reference(x_words, x_scales, w1_words, w1_scales, w2_words, w2_scales, gs, d_words, d_scales, mem, offs, hz, n1, n2, k1, n3):
    d_k1 = unpack_weight(d_words, d_scales)[np.arange(K)[:, None], runs(k1, K)]
    xq = unpack_weight(x_words, x_scales)[np.arange(K)[:, None], runs(offs, K)]
    x_hz = unpack_weight(x_words, x_scales)[np.arange(K)[:, None], runs(hz, K)]
    y = unpack_fp4(w1_words, w1_scales).T @ xq + unpack_fp4(w2_words, w2_scales).T @ x_hz
    st = np.maximum(y, y[np.arange(H)[:, None], runs(n1, H)])
    ds = np.zeros((H, S))
    ds[np.arange(H)[:, None], runs(n2, H)] = st
    z = f64(gs) * (ds - y)
    h = 0.0625 * ((d_k1.T @ mxq(z, 0, "e4m3")))
    nw = np.maximum(h, 0.5 * (f64(mem)[np.arange(H)[:, None], runs(n3, H)]))
    out = f64(mem).copy()
    out[np.arange(H)[:, None], runs(n3, H)] = nw
    return out

@@ -1,0 +1,219 @@
+from contextlib import ExitStack
+
+import concourse.mybir as mybir
+
+K, T, S, H, G, U = 512, 1024, 512, 512, 2048, 1024
+FLOPS = 2 * 3 * K * H * S
+
+F32 = mybir.dt.float32
+BF16 = mybir.dt.bfloat16
+I32 = mybir.dt.int32
+U32 = mybir.dt.uint32
+U16 = mybir.dt.uint16
+U8 = mybir.dt.uint8
+FP8X4 = mybir.dt.float8_e4m3fn_x4
+FP4X4 = mybir.dt.float4_e2m1fn_x4
+ALU = mybir.AluOpType
+COPY = mybir.ActivationFunctionType.Copy
+
+P = 128
+PACK = 4
+CHUNK = 128
+
+
+def tile_picked_dhqsendhoppagex_none_p_kernel(
+    tc, x_words, x_scales, w1_words, w1_scales, w2_words, w2_scales, gs, d_words, d_scales, mem, offs, hz, n1, n2, k1, n3, out
+):
+    nc = tc.nc
+    with ExitStack() as ctx:
+        lists = ctx.enter_context(tc.tile_pool(name="lists", bufs=1))
+        keep = ctx.enter_context(tc.tile_pool(name="keep", bufs=1))
+        reuse = ctx.enter_context(tc.tile_pool(name="reuse", bufs=1))
+        psum = ctx.enter_context(tc.psum_pool(name="psum", bufs=1))
+
+        def load_list(src, name):
+            tile = lists.tile([P, S // 16], U16, name=name)
+            nc.sync.dma_start(tile[:], src)
+            return tile
+
+        def zeroed_bytes(width, name, tag):
+            tile = keep.tile([P, width], U8, name=name, tag=tag, align_bytes=64)
+            nc.vector.memset(tile[:].bitcast(I32), 0)
+            return tile
+
+        def place_scale_rows(dst, src):
+            for q in range(4):
+                nc.sync.dma_start(dst[32 * q : 32 * q + 4, :].bitcast(I32), src[32 * q : 32 * q + 32 : 8, :].bitcast(I32))
+
+        x_byte_table = reuse.tile([P, T], U8, name="x_byte_table", offset=4 * T, align_bytes=64)
+        w_rows = zeroed_bytes(2 * H, "w_rows", "w_rows")
+        d_byte_table = zeroed_bytes(G, "d_byte_table", "d_byte_table")
+        x_plane = zeroed_bytes(2 * S, "x_plane", "page1")
+        d_plane = zeroed_bytes(H, "d_plane", "d_plane")
+
+        offs_sb = load_list(offs, "offs_sb")
+        nc.sync.dma_start(x_byte_table[:].bitcast(I32), x_scales[0].bitcast(I32).unsqueeze(1).to_broadcast([16, 8, T // 4]))
+        hz_sb = load_list(hz, "hz_sb")
+        x_word_table = reuse.tile([P, T], I32, name="x_word_table", offset=0, align_bytes=64)
+        nc.sync.dma_start(x_word_table[:], x_words[0].rearrange("p c r -> p (c r)").bitcast(I32))
+        w_bytes_raw = keep.tile([P, 2, 64], U8, name="w_bytes_raw", align_bytes=64)
+        for i, scales in enumerate((w1_scales, w2_scales)):
+            nc.scalar.dma_start(w_bytes_raw[:, i, :].bitcast(I32), scales[0].rearrange("r (e b) -> (r e) b", e=8).bitcast(I32))
+        w_bytes_part = keep.tile([P, 2 * 64], U8, name="w_bytes_part", align_bytes=64)
+        nc.vector.tensor_copy(
+            w_bytes_part[:].rearrange("p (w t m) -> p w t m", w=2, t=PACK),
+            w_bytes_raw[:].rearrange("p w (m t) -> p w t m", t=PACK),
+        )
+        for q in range(4):
+            nc.scalar.dma_start(w_rows[32 * q : 32 * q + 4, :].bitcast(I32), w_bytes_part[32 * q : 32 * q + 32, :].bitcast(I32))
+        gs_sb = keep.tile([P, PACK], F32, name="gs_sb")
+        nc.gpsimd.dma_start(gs_sb[:], gs.rearrange("(p t) o -> p (t o)", t=PACK))
+        w_raw = []
+        for name, words in (("w1_raw", w1_words), ("w2_raw", w2_words)):
+            tile = keep.tile([P, 2 * H], U8, name=name, align_bytes=64)
+            nc.sync.dma_start(tile[:].bitcast(I32), words[0].bitcast(I32))
+            w_raw.append(tile)
+        k1_sb = load_list(k1, "k1_sb")
+        nc.gpsimd.dma_start(d_byte_table[0:P:8, :].bitcast(I32), d_scales[0].bitcast(I32))
+        n1_sb = load_list(n1, "n1_sb")
+        n2_sb = load_list(n2, "n2_sb")
+        n3_sb = load_list(n3, "n3_sb")
+
+        neg_gs = keep.tile([P, PACK], F32, name="neg_gs")
+        nc.scalar.activation(neg_gs[:], gs_sb[:], COPY, scale=-1.0)
+
+        x_bytes = keep.tile([P, 2 * S], U8, name="x_bytes", tag="page0", align_bytes=64)
+        nc.vector.tensor_copy(x_bytes[:, 0:S], x_byte_table[:].indirect(offs_sb[:]))
+        nc.vector.tensor_copy(x_bytes[:, S : 2 * S], x_byte_table[:].indirect(hz_sb[:]))
+        place_scale_rows(x_plane, x_bytes)
+        d_word_table = reuse.tile([P, G], I32, name="d_word_table", offset=4 * T, align_bytes=64)
+        nc.sync.dma_start(d_word_table[:], d_words[0].rearrange("p c r -> p (c r)").bitcast(I32))
+
+        w_plane = keep.tile([P, 2 * H], U8, name="w_plane", tag="page2", align_bytes=64)
+        nc.scalar.copy(
+            w_plane[:].bitcast(U32).rearrange("p (b e m) -> p b e m", b=2 * PACK, e=8),
+            w_rows[:].bitcast(U32).rearrange("p (e b m) -> p b e m", b=2 * PACK, e=8),
+        )
+        w_codes = []
+        for i in range(2):
+            tile = keep.tile([P, 2 * H], U8, name="w_codes%d" % i, align_bytes=64)
+            nc.scalar.copy(
+                tile[:].bitcast(U16).rearrange("p (t m) -> p t m", t=PACK),
+                w_raw[i][:].bitcast(U16).rearrange("p (m t) -> p t m", t=PACK),
+            )
+            w_codes.append(tile)
+
+        x_codes = []
+        for i, lst in enumerate((offs_sb, hz_sb)):
+            tile = keep.tile([P, S], U32, name="x_codes%d" % i, tag=("page3", "x_codes1")[i], align_bytes=64)
+            nc.vector.tensor_copy(tile[:], x_word_table[:].bitcast(U32).indirect(lst[:]))
+            x_codes.append(tile)
+
+        y_ps = [psum.tile([P, S], F32, name="y_ps%d" % t, tag="bank%d" % t) for t in range(PACK)]
+        for t in range(PACK):
+            for i in range(2):
+                nc.tensor.matmul_mx(
+                    y_ps[t][:],
+                    lhsT=w_codes[i][:, 2 * P * t : 2 * P * (t + 1)].bitcast(FP4X4),
+                    lhsT_scale=w_plane[:, i * H + P * t : i * H + P * (t + 1)],
+                    rhs=x_codes[i][:].bitcast(FP8X4),
+                    rhs_scale=x_plane[:, i * S : (i + 1) * S],
+                    start=(i == 0),
+                    stop=(i == 1),
+                )
+
+        d_bytes = reuse.tile([P, H], U8, name="d_bytes", offset=4 * H, align_bytes=64)
+        nc.vector.tensor_copy(d_bytes[:], d_byte_table[:].indirect(k1_sb[:]))
+        d_picked = reuse.tile([P, H], U32, name="d_picked", offset=0, align_bytes=64)
+        nc.vector.tensor_copy(d_picked[:], d_word_table[:].bitcast(U32).indirect(k1_sb[:]))
+        d_bytes_dealt = keep.tile([P, H], U8, name="d_bytes_dealt", align_bytes=64)
+        nc.vector.tensor_copy(
+            d_bytes_dealt[:].rearrange("p (t m) -> p t m", t=PACK), d_bytes[:].rearrange("p (m t) -> p t m", t=PACK)
+        )
+        place_scale_rows(d_plane, d_bytes_dealt)
+
+        mem_rows = mem.rearrange("(p t) c -> t p c", t=PACK)
+        out_rows = out.rearrange("(p t) c -> t p c", t=PACK)
+        page = []
+        for t in range(PACK):
+            tile = keep.tile([P, U], F32, name="page%d" % t, tag="page%d" % t, align_bytes=64)
+            nc.sync.dma_start(tile[:], mem_rows[t])
+            page.append(tile)
+
+        z32 = keep.tile([P, PACK, S], F32, name="z32")
+        half = S // 2
+        sent = []
+
+        def fetch_and_send(t):
+            y_sb = keep.tile([P, S], F32, name="y_sb%d" % t, tag="y_sb%d" % t)
+            nc.scalar.copy(y_sb[:], y_ps[t][:])
+            fetched = keep.tile([P, S], F32, name="fetched%d" % t)
+            for a in range(0, S, half):
+                nc.scalar.activation(fetched[:, a : a + half], y_sb[:].indirect(n1_sb[:, a // 16 : (a + half) // 16]), COPY)
+            st = keep.tile([P, S], F32, name="st%d" % t, tag="st%d" % t, align_bytes=64)
+            ds = keep.tile([P, 2 * S], F32, name="ds%d" % t)
+            step = half if t == 0 else S
+            for a in range(0, S, step):
+                nc.vector.tensor_tensor(st[:, a : a + step], y_ps[t][:, a : a + step], fetched[:, a : a + step], ALU.max)
+                nc.vector.tensor_copy(ds[:].indirect(n2_sb[:, a // 16 : (a + step) // 16]), st[:, a : a + step])
+            sent.append(ds)
+
+        def weigh(t):
+            ngy = keep.tile([P, S], F32, name="neg_gy%d" % t, tag="y_sb%d" % ((t + 1) % PACK))
+            nc.scalar.activation(ngy[:], y_ps[t][:], COPY, scale=neg_gs[:, t : t + 1])
+            step = CHUNK if t == PACK - 1 else S
+            for a in range(0, S, step):
+                nc.vector.scalar_tensor_tensor(
+                    z32[:, t, a : a + step], sent[t][:, a : a + step], gs_sb[:, t : t + 1], ngy[:, a : a + step], ALU.mult, ALU.add
+                )
+
+        fetch_and_send(0)
+        for t in range(1, PACK):
+            fetch_and_send(t)
+            if t < PACK - 1:
+                weigh(t - 1)
+        weigh(PACK - 2)
+        weigh(PACK - 1)
+        d_codes = keep.tile([P, H], U32, name="d_codes", tag="st3", align_bytes=64)
+        nc.vector.tensor_copy(
+            d_codes[:].rearrange("p (t m) -> p m t", t=PACK), d_picked[:].rearrange("p (m t) -> p m t", t=PACK)
+        )
+
+        held = []
+        for t in range(PACK):
+            tile = keep.tile([P, S], F32, name="held%d" % t)
+            nc.scalar.activation(tile[:], page[t][:].indirect(n3_sb[:]), COPY, scale=0.5)
+            held.append(tile)
+
+        z_codes = keep.tile([P, S], U32, name="z_codes", align_bytes=64)
+        z_plane = keep.tile([P, S], U8, name="z_plane", align_bytes=64)
+        nw = [keep.tile([P, S], F32, name="nw%d" % t) for t in range(PACK)]
+
+        def second_product(t, bank, a, width):
+            h_ps = psum.tile([P, width], F32, name="h_ps", tag="bank%d" % bank)
+            nc.tensor.matmul_mx(
+                h_ps[:],
+                lhsT=d_codes[:, P * t : P * (t + 1)].bitcast(FP8X4),
+                lhsT_scale=d_plane[:, P * t : P * (t + 1)],
+                rhs=z_codes[:, a : a + width].bitcast(FP8X4),
+                rhs_scale=z_plane[:, a : a + width],
+                start=True,
+                stop=True,
+            )
+            nc.vector.scalar_tensor_tensor(nw[t][:, a : a + width], h_ps[:], 0.0625, held[t][:, a : a + width], ALU.mult, ALU.max)
+            nc.vector.tensor_copy(page[t][:].indirect(n3_sb[:, a // 16 : (a + width) // 16]), nw[t][:, a : a + width])
+
+        for c in range(S // CHUNK):
+            a = c * CHUNK
+            z16 = keep.tile([P, CHUNK, PACK], BF16, name="z16_%d" % c, align_bytes=64)
+            nc.scalar.copy(z16[:], z32[:, :, a : a + CHUNK].rearrange("p t j -> p j t"))
+            nc.vector.quantize_mx(
+                z_codes[:, a : a + CHUNK].bitcast(FP8X4), z_plane[:, a : a + CHUNK], z16[:].rearrange("p j t -> p (j t)")
+            )
+            if c < 2:
+                second_product(0, c, a, CHUNK)
+        second_product(0, 2, 2 * CHUNK, 2 * CHUNK)
+        nc.sync.dma_start(out_rows[0], page[0][:])
+        for t in range(1, PACK):
+            second_product(t, PACK + t, 0, S)
+            nc.sync.dma_start(out_rows[t], page[t][:])

@@ -15,6 +15,7 @@ FP8X4 = mybir.dt.float8_e4m3fn_x4
 FP4X4 = mybir.dt.float4_e2m1fn_x4
 ALU = mybir.AluOpType
 COPY = mybir.ActivationFunctionType.Copy
+RELU = mybir.ActivationFunctionType.Relu
 
 P = 128
 PACK = 4
@@ -73,12 +74,10 @@ def tile_picked_dhqsendhoppagex_none_p_kernel(
             tile = keep.tile([P, 2 * H], U8, name=name, align_bytes=64)
             nc.sync.dma_start(tile[:].bitcast(I32), words[0].bitcast(I32))
             w_raw.append(tile)
-        k1_sb = load_list(k1, "k1_sb")
         nc.gpsimd.dma_start(d_byte_table[0:P:8, :].bitcast(I32), d_scales[0].bitcast(I32))
-        n1_sb = load_list(n1, "n1_sb")
-        n2_sb = load_list(n2, "n2_sb")
-        n3_sb = load_list(n3, "n3_sb")
 
+        d_word_table = keep.tile([P, G], I32, name="d_word_table", align_bytes=64)
+        nc.gpsimd.dma_start(d_word_table[:], d_words[0].rearrange("p c r -> p (c r)").bitcast(I32))
         neg_gs = keep.tile([P, PACK], F32, name="neg_gs")
         nc.scalar.activation(neg_gs[:], gs_sb[:], COPY, scale=-1.0)
 
@@ -86,8 +85,6 @@ def tile_picked_dhqsendhoppagex_none_p_kernel(
         nc.vector.tensor_copy(x_bytes[:, 0:S], x_byte_table[:].indirect(offs_sb[:]))
         nc.vector.tensor_copy(x_bytes[:, S : 2 * S], x_byte_table[:].indirect(hz_sb[:]))
         place_scale_rows(x_plane, x_bytes)
-        d_word_table = reuse.tile([P, G], I32, name="d_word_table", offset=4 * T, align_bytes=64)
-        nc.sync.dma_start(d_word_table[:], d_words[0].rearrange("p c r -> p (c r)").bitcast(I32))
 
         w_plane = keep.tile([P, 2 * H], U8, name="w_plane", tag="page2", align_bytes=64)
         nc.scalar.copy(
@@ -122,6 +119,10 @@ def tile_picked_dhqsendhoppagex_none_p_kernel(
                     stop=(i == 1),
                 )
 
+        k1_sb = load_list(k1, "k1_sb")
+        n1_sb = load_list(n1, "n1_sb")
+        n2_sb = load_list(n2, "n2_sb")
+        n3_sb = load_list(n3, "n3_sb")
         d_bytes = reuse.tile([P, H], U8, name="d_bytes", offset=4 * H, align_bytes=64)
         nc.vector.tensor_copy(d_bytes[:], d_byte_table[:].indirect(k1_sb[:]))
         d_picked = reuse.tile([P, H], U32, name="d_picked", offset=0, align_bytes=64)
@@ -140,56 +141,76 @@ def tile_picked_dhqsendhoppagex_none_p_kernel(
             nc.sync.dma_start(tile[:], mem_rows[t])
             page.append(tile)
 
-        z32 = keep.tile([P, PACK, S], F32, name="z32")
+        z32 = reuse.tile([P, PACK, S], F32, name="z32", offset=8 * T, align_bytes=64)
         half = S // 2
         sent = []
+        y_sb = []
+
+        def work_tile(width, name, tag):
+            return keep.tile([P, width], F32, name=name, tag=tag, align_bytes=64)
+
+        def larger_on_gpsimd(out_ap, low, other, key):
+            gap = work_tile(out_ap.shape[1], "gap", "gap" + key)
+            nc.gpsimd.tensor_tensor(gap[:], other, low, ALU.subtract)
+            rise = work_tile(out_ap.shape[1], "rise", "rise" + key)
+            nc.scalar.activation(rise[:], gap[:], RELU)
+            nc.gpsimd.tensor_tensor(out_ap, low, rise[:], ALU.add)
 
         def fetch_and_send(t):
-            y_sb = keep.tile([P, S], F32, name="y_sb%d" % t, tag="y_sb%d" % t)
-            nc.scalar.copy(y_sb[:], y_ps[t][:])
-            fetched = keep.tile([P, S], F32, name="fetched%d" % t)
-            for a in range(0, S, half):
-                nc.scalar.activation(fetched[:, a : a + half], y_sb[:].indirect(n1_sb[:, a // 16 : (a + half) // 16]), COPY)
-            st = keep.tile([P, S], F32, name="st%d" % t, tag="st%d" % t, align_bytes=64)
+            y = work_tile(S, "y_sb", "fetched00" if t == 1 else "y_sb%d" % t)
+            y_sb.append(y)
+            nc.scalar.copy(y[:], y_ps[t][:])
+            st = work_tile(S, "st", "st%d" % t)
             ds = keep.tile([P, 2 * S], F32, name="ds%d" % t)
-            step = half if t == 0 else S
-            for a in range(0, S, step):
-                nc.vector.tensor_tensor(st[:, a : a + step], y_ps[t][:, a : a + step], fetched[:, a : a + step], ALU.max)
-                nc.vector.tensor_copy(ds[:].indirect(n2_sb[:, a // 16 : (a + step) // 16]), st[:, a : a + step])
             sent.append(ds)
+            if t == 1:
+                fetched = work_tile(S, "fetched", "fetched1")
+                for a in range(0, S, half):
+                    nc.scalar.activation(fetched[:, a : a + half], y[:].indirect(n1_sb[:, a // 16 : (a + half) // 16]), COPY)
+                nc.vector.tensor_tensor(st[:], y_ps[t][:], fetched[:], ALU.max)
+            else:
+                for i in range(2):
+                    a = i * half
+                    fetched = work_tile(half, "fetched", "fetched%d%d" % (t, i))
+                    nc.scalar.activation(fetched[:], y[:].indirect(n1_sb[:, a // 16 : (a + half) // 16]), COPY)
+                    if t == 0:
+                        nc.vector.tensor_tensor(st[:, a : a + half], y_ps[t][:, a : a + half], fetched[:], ALU.max)
+                        nc.vector.tensor_copy(ds[:].indirect(n2_sb[:, a // 16 : (a + half) // 16]), st[:, a : a + half])
+                    else:
+                        larger_on_gpsimd(st[:, a : a + half], y[:, a : a + half], fetched[:], "%d%d" % (t, i))
+            if t > 0:
+                nc.vector.tensor_copy(ds[:].indirect(n2_sb[:]), st[:])
 
-        def weigh(t):
-            ngy = keep.tile([P, S], F32, name="neg_gy%d" % t, tag="y_sb%d" % ((t + 1) % PACK))
-            nc.scalar.activation(ngy[:], y_ps[t][:], COPY, scale=neg_gs[:, t : t + 1])
-            step = CHUNK if t == PACK - 1 else S
-            for a in range(0, S, step):
-                nc.vector.scalar_tensor_tensor(
-                    z32[:, t, a : a + step], sent[t][:, a : a + step], gs_sb[:, t : t + 1], ngy[:, a : a + step], ALU.mult, ALU.add
-                )
-
-        fetch_and_send(0)
-        for t in range(1, PACK):
+        for t in range(PACK):
             fetch_and_send(t)
-            if t < PACK - 1:
-                weigh(t - 1)
-        weigh(PACK - 2)
-        weigh(PACK - 1)
-        d_codes = keep.tile([P, H], U32, name="d_codes", tag="st3", align_bytes=64)
+        for t, tag in enumerate(("rise21", "rise30", "rise31")):
+            diff = work_tile(S, "diff", tag)
+            nc.gpsimd.tensor_tensor(diff[:], sent[t][:, 0:S], y_sb[t][:], ALU.subtract)
+            nc.scalar.activation(z32[:, t, :], diff[:], COPY, scale=gs_sb[:, t : t + 1])
+        last = PACK - 1
+        ngy = work_tile(S, "neg_gy", "gap30")
+        nc.scalar.activation(ngy[:], y_ps[last][:], COPY, scale=neg_gs[:, last : last + 1])
+        for a in range(0, S, CHUNK):
+            nc.vector.scalar_tensor_tensor(
+                z32[:, last, a : a + CHUNK], sent[last][:, a : a + CHUNK], gs_sb[:, last : last + 1], ngy[:, a : a + CHUNK], ALU.mult, ALU.add
+            )
+        d_codes = keep.tile([P, H], U32, name="d_codes", tag="st2", align_bytes=64)
         nc.vector.tensor_copy(
             d_codes[:].rearrange("p (t m) -> p m t", t=PACK), d_picked[:].rearrange("p (m t) -> p m t", t=PACK)
         )
 
         held = []
-        for t in range(PACK):
-            tile = keep.tile([P, S], F32, name="held%d" % t)
+
+        def fetch_held(t, tile):
             nc.scalar.activation(tile[:], page[t][:].indirect(n3_sb[:]), COPY, scale=0.5)
             held.append(tile)
 
+        fetch_held(0, work_tile(S, "held0", "gap31"))
+
         z_codes = keep.tile([P, S], U32, name="z_codes", align_bytes=64)
         z_plane = keep.tile([P, S], U8, name="z_plane", align_bytes=64)
-        nw = [keep.tile([P, S], F32, name="nw%d" % t) for t in range(PACK)]
 
-        def second_product(t, bank, a, width):
+        def second_product(t, bank, a, width, tag):
             h_ps = psum.tile([P, width], F32, name="h_ps", tag="bank%d" % bank)
             nc.tensor.matmul_mx(
                 h_ps[:],
@@ -200,20 +221,28 @@ def tile_picked_dhqsendhoppagex_none_p_kernel(
                 start=True,
                 stop=True,
             )
-            nc.vector.scalar_tensor_tensor(nw[t][:, a : a + width], h_ps[:], 0.0625, held[t][:, a : a + width], ALU.mult, ALU.max)
-            nc.vector.tensor_copy(page[t][:].indirect(n3_sb[:, a // 16 : (a + width) // 16]), nw[t][:, a : a + width])
+            nw = keep.tile([P, width], F32, name="nw", tag=tag, align_bytes=64)
+            if t < 2:
+                nc.vector.scalar_tensor_tensor(nw[:], h_ps[:], 0.0625, held[t][:, a : a + width], ALU.mult, ALU.max)
+            else:
+                h = work_tile(width, "h", "h%d" % t)
+                nc.scalar.activation(h[:], h_ps[:], COPY, scale=0.0625)
+                larger_on_gpsimd(nw[:], h[:], held[t][:], "h%d" % t)
+            nc.vector.tensor_copy(page[t][:].indirect(n3_sb[:, a // 16 : (a + width) // 16]), nw[:])
 
         for c in range(S // CHUNK):
             a = c * CHUNK
-            z16 = keep.tile([P, CHUNK, PACK], BF16, name="z16_%d" % c, align_bytes=64)
+            z16 = keep.tile([P, CHUNK, PACK], BF16, name="z16_%d" % c, tag="z16_%d" % c, align_bytes=64)
             nc.scalar.copy(z16[:], z32[:, :, a : a + CHUNK].rearrange("p t j -> p j t"))
             nc.vector.quantize_mx(
                 z_codes[:, a : a + CHUNK].bitcast(FP8X4), z_plane[:, a : a + CHUNK], z16[:].rearrange("p j t -> p (j t)")
             )
-            if c < 2:
-                second_product(0, c, a, CHUNK)
-        second_product(0, 2, 2 * CHUNK, 2 * CHUNK)
+        for t in range(1, PACK):
+            fetch_held(t, reuse.tile([P, S], F32, name="held%d" % t, offset=8 * T + 4 * S * t, align_bytes=64))
+        second_product(0, 0, 0, CHUNK, "z16_1")
+        second_product(0, 1, CHUNK, CHUNK, "z16_3")
+        second_product(0, 2, 2 * CHUNK, 2 * CHUNK, "nw0")
         nc.sync.dma_start(out_rows[0], page[0][:])
         for t in range(1, PACK):
-            second_product(t, PACK + t, 0, S)
+            second_product(t, PACK + t, 0, S, "nw%d" % t)
             nc.sync.dma_start(out_rows[t], page[t][:])

@@ -76,8 +76,6 @@ def tile_picked_dhqsendhoppagex_none_p_kernel(
             w_raw.append(tile)
         nc.gpsimd.dma_start(d_byte_table[0:P:8, :].bitcast(I32), d_scales[0].bitcast(I32))
 
-        d_word_table = keep.tile([P, G], I32, name="d_word_table", align_bytes=64)
-        nc.gpsimd.dma_start(d_word_table[:], d_words[0].rearrange("p c r -> p (c r)").bitcast(I32))
         neg_gs = keep.tile([P, PACK], F32, name="neg_gs")
         nc.scalar.activation(neg_gs[:], gs_sb[:], COPY, scale=-1.0)
 
@@ -106,33 +104,39 @@ def tile_picked_dhqsendhoppagex_none_p_kernel(
             nc.vector.tensor_copy(tile[:], x_word_table[:].bitcast(U32).indirect(lst[:]))
             x_codes.append(tile)
 
-        y_ps = [psum.tile([P, S], F32, name="y_ps%d" % t, tag="bank%d" % t) for t in range(PACK)]
-        for t in range(PACK):
+        half = S // 2
+
+        def first_product(t, bank, a, width):
+            y_bank = psum.tile([P, width], F32, name="y_bank", tag="bank%d" % bank)
             for i in range(2):
                 nc.tensor.matmul_mx(
-                    y_ps[t][:],
+                    y_bank[:],
                     lhsT=w_codes[i][:, 2 * P * t : 2 * P * (t + 1)].bitcast(FP4X4),
                     lhsT_scale=w_plane[:, i * H + P * t : i * H + P * (t + 1)],
-                    rhs=x_codes[i][:].bitcast(FP8X4),
-                    rhs_scale=x_plane[:, i * S : (i + 1) * S],
+                    rhs=x_codes[i][:, a : a + width].bitcast(FP8X4),
+                    rhs_scale=x_plane[:, i * S + a : i * S + a + width],
                     start=(i == 0),
                     stop=(i == 1),
                 )
+            return y_bank
+
+        y_first = [first_product(0, 0, 0, half), first_product(0, PACK, half, half)]
+        y_ps = [None] + [first_product(t, t, 0, S) for t in range(1, PACK)]
 
         k1_sb = load_list(k1, "k1_sb")
         n1_sb = load_list(n1, "n1_sb")
         n2_sb = load_list(n2, "n2_sb")
         n3_sb = load_list(n3, "n3_sb")
-        d_bytes = reuse.tile([P, H], U8, name="d_bytes", offset=4 * H, align_bytes=64)
+        d_bytes = reuse.tile([P, H], U8, name="d_bytes", offset=0, align_bytes=64)
         nc.vector.tensor_copy(d_bytes[:], d_byte_table[:].indirect(k1_sb[:]))
-        d_picked = reuse.tile([P, H], U32, name="d_picked", offset=0, align_bytes=64)
-        nc.vector.tensor_copy(d_picked[:], d_word_table[:].bitcast(U32).indirect(k1_sb[:]))
         d_bytes_dealt = keep.tile([P, H], U8, name="d_bytes_dealt", align_bytes=64)
         nc.vector.tensor_copy(
             d_bytes_dealt[:].rearrange("p (t m) -> p t m", t=PACK), d_bytes[:].rearrange("p (m t) -> p t m", t=PACK)
         )
         place_scale_rows(d_plane, d_bytes_dealt)
 
+        d_word_table = keep.tile([P, G], I32, name="d_word_table", tag="x_codes1", align_bytes=64)
+        nc.sync.dma_start(d_word_table[:], d_words[0].rearrange("p c r -> p (c r)").bitcast(I32))
         mem_rows = mem.rearrange("(p t) c -> t p c", t=PACK)
         out_rows = out.rearrange("(p t) c -> t p c", t=PACK)
         page = []
@@ -142,7 +146,6 @@ def tile_picked_dhqsendhoppagex_none_p_kernel(
             page.append(tile)
 
         z32 = reuse.tile([P, PACK, S], F32, name="z32", offset=8 * T, align_bytes=64)
-        half = S // 2
         sent = []
         y_sb = []
 
@@ -157,14 +160,18 @@ def tile_picked_dhqsendhoppagex_none_p_kernel(
             nc.gpsimd.tensor_tensor(out_ap, low, rise[:], ALU.add)
 
         def fetch_and_send(t):
-            y = work_tile(S, "y_sb", "fetched00" if t == 1 else "y_sb%d" % t)
+            y = work_tile(S, "y_sb", ("y_sb0", "fetched00", "fetched01", "fetched1")[t])
             y_sb.append(y)
-            nc.scalar.copy(y[:], y_ps[t][:])
+            if t == 0:
+                for i in range(2):
+                    nc.scalar.copy(y[:, i * half : (i + 1) * half], y_first[i][:])
+            else:
+                nc.scalar.copy(y[:], y_ps[t][:])
             st = work_tile(S, "st", "st%d" % t)
             ds = keep.tile([P, 2 * S], F32, name="ds%d" % t)
             sent.append(ds)
-            if t == 1:
-                fetched = work_tile(S, "fetched", "fetched1")
+            if t in (1, 2):
+                fetched = work_tile(S, "fetched", "fetched%d" % t)
                 for a in range(0, S, half):
                     nc.scalar.activation(fetched[:, a : a + half], y[:].indirect(n1_sb[:, a // 16 : (a + half) // 16]), COPY)
                 nc.vector.tensor_tensor(st[:], y_ps[t][:], fetched[:], ALU.max)
@@ -174,7 +181,7 @@ def tile_picked_dhqsendhoppagex_none_p_kernel(
                     fetched = work_tile(half, "fetched", "fetched%d%d" % (t, i))
                     nc.scalar.activation(fetched[:], y[:].indirect(n1_sb[:, a // 16 : (a + half) // 16]), COPY)
                     if t == 0:
-                        nc.vector.tensor_tensor(st[:, a : a + half], y_ps[t][:, a : a + half], fetched[:], ALU.max)
+                        nc.vector.tensor_tensor(st[:, a : a + half], y_first[i][:], fetched[:], ALU.max)
                         nc.vector.tensor_copy(ds[:].indirect(n2_sb[:, a // 16 : (a + half) // 16]), st[:, a : a + half])
                     else:
                         larger_on_gpsimd(st[:, a : a + half], y[:, a : a + half], fetched[:], "%d%d" % (t, i))
@@ -183,7 +190,7 @@ def tile_picked_dhqsendhoppagex_none_p_kernel(
 
         for t in range(PACK):
             fetch_and_send(t)
-        for t, tag in enumerate(("rise21", "rise30", "rise31")):
+        for t, tag in enumerate(("diff0", "rise30", "rise31")):
             diff = work_tile(S, "diff", tag)
             nc.gpsimd.tensor_tensor(diff[:], sent[t][:, 0:S], y_sb[t][:], ALU.subtract)
             nc.scalar.activation(z32[:, t, :], diff[:], COPY, scale=gs_sb[:, t : t + 1])
@@ -194,7 +201,9 @@ def tile_picked_dhqsendhoppagex_none_p_kernel(
             nc.vector.scalar_tensor_tensor(
                 z32[:, last, a : a + CHUNK], sent[last][:, a : a + CHUNK], gs_sb[:, last : last + 1], ngy[:, a : a + CHUNK], ALU.mult, ALU.add
             )
-        d_codes = keep.tile([P, H], U32, name="d_codes", tag="st2", align_bytes=64)
+        d_picked = keep.tile([P, H], U32, name="d_picked", tag="st3", align_bytes=64)
+        nc.vector.tensor_copy(d_picked[:], d_word_table[:].bitcast(U32).indirect(k1_sb[:]))
+        d_codes = keep.tile([P, H], U32, name="d_codes", align_bytes=64)
         nc.vector.tensor_copy(
             d_codes[:].rearrange("p (t m) -> p m t", t=PACK), d_picked[:].rearrange("p (m t) -> p m t", t=PACK)
         )
@@ -206,14 +215,15 @@ def tile_picked_dhqsendhoppagex_none_p_kernel(
             held.append(tile)
 
         fetch_held(0, work_tile(S, "held0", "gap31"))
+        fetch_held(1, work_tile(S, "held1", "rise30"))
 
         z_codes = keep.tile([P, S], U32, name="z_codes", align_bytes=64)
         z_plane = keep.tile([P, S], U8, name="z_plane", align_bytes=64)
 
-        def second_product(t, bank, a, width, tag):
-            h_ps = psum.tile([P, width], F32, name="h_ps", tag="bank%d" % bank)
+        def second_product(t, bank, a, width):
+            h_bank = psum.tile([P, width], F32, name="h_bank", tag="bank%d" % bank)
             nc.tensor.matmul_mx(
-                h_ps[:],
+                h_bank[:],
                 lhsT=d_codes[:, P * t : P * (t + 1)].bitcast(FP8X4),
                 lhsT_scale=d_plane[:, P * t : P * (t + 1)],
                 rhs=z_codes[:, a : a + width].bitcast(FP8X4),
@@ -221,12 +231,15 @@ def tile_picked_dhqsendhoppagex_none_p_kernel(
                 start=True,
                 stop=True,
             )
-            nw = keep.tile([P, width], F32, name="nw", tag=tag, align_bytes=64)
+            return h_bank
+
+        def write_back(t, h_bank, a, width, tag):
+            nw = work_tile(width, "nw", tag)
             if t < 2:
-                nc.vector.scalar_tensor_tensor(nw[:], h_ps[:], 0.0625, held[t][:, a : a + width], ALU.mult, ALU.max)
+                nc.vector.scalar_tensor_tensor(nw[:], h_bank[:], 0.0625, held[t][:, a : a + width], ALU.mult, ALU.max)
             else:
                 h = work_tile(width, "h", "h%d" % t)
-                nc.scalar.activation(h[:], h_ps[:], COPY, scale=0.0625)
+                nc.scalar.activation(h[:], h_bank[:], COPY, scale=0.0625)
                 larger_on_gpsimd(nw[:], h[:], held[t][:], "h%d" % t)
             nc.vector.tensor_copy(page[t][:].indirect(n3_sb[:, a // 16 : (a + width) // 16]), nw[:])
 
@@ -237,12 +250,13 @@ def tile_picked_dhqsendhoppagex_none_p_kernel(
             nc.vector.quantize_mx(
                 z_codes[:, a : a + CHUNK].bitcast(FP8X4), z_plane[:, a : a + CHUNK], z16[:].rearrange("p j t -> p (j t)")
             )
-        for t in range(1, PACK):
+        for t in range(2, PACK):
             fetch_held(t, reuse.tile([P, S], F32, name="held%d" % t, offset=8 * T + 4 * S * t, align_bytes=64))
-        second_product(0, 0, 0, CHUNK, "z16_1")
-        second_product(0, 1, CHUNK, CHUNK, "z16_3")
-        second_product(0, 2, 2 * CHUNK, 2 * CHUNK, "nw0")
+        h_first = [second_product(0, 0, 0, half), second_product(0, 1, half, half)]
+        h_ps = {t: second_product(t, PACK + t, 0, S) for t in (2, 1, 3)}
+        write_back(0, h_first[0], 0, half, "z16_2")
+        write_back(0, h_first[1], half, half, "nw0")
         nc.sync.dma_start(out_rows[0], page[0][:])
         for t in range(1, PACK):
-            second_product(t, PACK + t, 0, S, "nw%d" % t)
+            write_back(t, h_ps[t], 0, S, "nw%d" % t)
             nc.sync.dma_start(out_rows[t], page[t][:])

@@ -205,7 +205,7 @@ def tile_picked_dhqsendhoppagex_none_p_kernel(
         nc.vector.tensor_copy(d_picked[:], d_word_table[:].bitcast(U32).indirect(k1_sb[:]))
         d_codes = keep.tile([P, H], U32, name="d_codes", align_bytes=64)
         nc.vector.tensor_copy(
-            d_codes[:].rearrange("p (t m) -> p m t", t=PACK), d_picked[:].rearrange("p (m t) -> p m t", t=PACK)
+            d_codes[:].rearrange("p (t c i) -> p c t i", t=PACK, i=4), d_picked[:].rearrange("p (c i t) -> p c t i", t=PACK, i=4)
         )
 
         held = []
@@ -246,17 +246,24 @@ def tile_picked_dhqsendhoppagex_none_p_kernel(
         for c in range(S // CHUNK):
             a = c * CHUNK
             z16 = keep.tile([P, CHUNK, PACK], BF16, name="z16_%d" % c, tag="z16_%d" % c, align_bytes=64)
-            nc.scalar.copy(z16[:], z32[:, :, a : a + CHUNK].rearrange("p t j -> p j t"))
+            nc.scalar.copy(
+                z16[:].rearrange("p (c i) t -> p c t i", i=4), z32[:, :, a : a + CHUNK].rearrange("p t (c i) -> p c t i", i=4)
+            )
             nc.vector.quantize_mx(
                 z_codes[:, a : a + CHUNK].bitcast(FP8X4), z_plane[:, a : a + CHUNK], z16[:].rearrange("p j t -> p (j t)")
             )
         for t in range(2, PACK):
             fetch_held(t, reuse.tile([P, S], F32, name="held%d" % t, offset=8 * T + 4 * S * t, align_bytes=64))
-        h_first = [second_product(0, 0, 0, half), second_product(0, 1, half, half)]
-        h_ps = {t: second_product(t, PACK + t, 0, S) for t in (2, 1, 3)}
+        h_first = [second_product(0, 0, 0, half)]
+        h_ps = {1: second_product(1, PACK + 1, 0, S)}
+        h_first.append(second_product(0, 1, half, half))
+        for t in range(2, PACK):
+            h_ps[t] = second_product(t, PACK + t, 0, S)
         write_back(0, h_first[0], 0, half, "z16_2")
+        write_back(1, h_ps[1], 0, S, "nw1")
+        nc.sync.dma_start(out_rows[1], page[1][:])
         write_back(0, h_first[1], half, half, "nw0")
         nc.sync.dma_start(out_rows[0], page[0][:])
-        for t in range(1, PACK):
+        for t in range(2, PACK):
             write_back(t, h_ps[t], 0, S, "nw%d" % t)
             nc.sync.dma_start(out_rows[t], page[t][:])

@@ -19,7 +19,19 @@ RELU = mybir.ActivationFunctionType.Relu
 
 P = 128
 PACK = 4
+LAST = PACK - 1
+QUADRANTS = 4
+BLOCK_PARTITIONS = 8
+BLOCK_ROWS = P // BLOCK_PARTITIONS
+PER_COLUMN = 16
+HALF = S // 2
 CHUNK = 128
+LINE = 4
+SEGMENT = H // BLOCK_PARTITIONS
+
+X_WORDS_AT = 0
+X_BYTES_AT = 4 * T
+Z_AT = 8 * T
 
 
 def tile_picked_dhqsendhoppagex_none_p_kernel(
@@ -33,39 +45,52 @@ def tile_picked_dhqsendhoppagex_none_p_kernel(
         psum = ctx.enter_context(tc.psum_pool(name="psum", bufs=1))
 
         def load_list(src, name):
-            tile = lists.tile([P, S // 16], U16, name=name)
+            tile = lists.tile([P, S // PER_COLUMN], U16, name=name)
             nc.sync.dma_start(tile[:], src)
             return tile
+
+        def entries(list_tile, first, count):
+            return list_tile[:, first // PER_COLUMN : (first + count) // PER_COLUMN]
 
         def zeroed_bytes(width, name, tag):
             tile = keep.tile([P, width], U8, name=name, tag=tag, align_bytes=64)
             nc.vector.memset(tile[:].bitcast(I32), 0)
             return tile
 
-        def place_scale_rows(dst, src):
-            for q in range(4):
-                nc.sync.dma_start(dst[32 * q : 32 * q + 4, :].bitcast(I32), src[32 * q : 32 * q + 32 : 8, :].bitcast(I32))
+        def place_scale_rows(plane, picked):
+            for q in range(QUADRANTS):
+                nc.sync.dma_start(
+                    plane[32 * q : 32 * q + 4, :].bitcast(I32), picked[32 * q : 32 * q + 32 : BLOCK_PARTITIONS, :].bitcast(I32)
+                )
 
-        x_byte_table = reuse.tile([P, T], U8, name="x_byte_table", offset=4 * T, align_bytes=64)
+        def work_tile(width, name, tag):
+            return keep.tile([P, width], F32, name=name, tag=tag, align_bytes=64)
+
+        x_byte_table = reuse.tile([P, T], U8, name="x_byte_table", offset=X_BYTES_AT, align_bytes=64)
         w_rows = zeroed_bytes(2 * H, "w_rows", "w_rows")
         d_byte_table = zeroed_bytes(G, "d_byte_table", "d_byte_table")
         x_plane = zeroed_bytes(2 * S, "x_plane", "page1")
         d_plane = zeroed_bytes(H, "d_plane", "d_plane")
 
         offs_sb = load_list(offs, "offs_sb")
-        nc.sync.dma_start(x_byte_table[:].bitcast(I32), x_scales[0].bitcast(I32).unsqueeze(1).to_broadcast([16, 8, T // 4]))
+        nc.sync.dma_start(
+            x_byte_table[:].bitcast(I32), x_scales[0].bitcast(I32).unsqueeze(1).to_broadcast([BLOCK_ROWS, BLOCK_PARTITIONS, T // 4])
+        )
         hz_sb = load_list(hz, "hz_sb")
-        x_word_table = reuse.tile([P, T], I32, name="x_word_table", offset=0, align_bytes=64)
+        x_word_table = reuse.tile([P, T], I32, name="x_word_table", offset=X_WORDS_AT, align_bytes=64)
         nc.sync.dma_start(x_word_table[:], x_words[0].rearrange("p c r -> p (c r)").bitcast(I32))
-        w_bytes_raw = keep.tile([P, 2, 64], U8, name="w_bytes_raw", align_bytes=64)
+
+        w_bytes_raw = keep.tile([P, 2, SEGMENT], U8, name="w_bytes_raw", align_bytes=64)
         for i, scales in enumerate((w1_scales, w2_scales)):
-            nc.scalar.dma_start(w_bytes_raw[:, i, :].bitcast(I32), scales[0].rearrange("r (e b) -> (r e) b", e=8).bitcast(I32))
-        w_bytes_part = keep.tile([P, 2 * 64], U8, name="w_bytes_part", align_bytes=64)
+            nc.scalar.dma_start(
+                w_bytes_raw[:, i, :].bitcast(I32), scales[0].rearrange("r (e b) -> (r e) b", e=BLOCK_PARTITIONS).bitcast(I32)
+            )
+        w_bytes_part = keep.tile([P, 2 * SEGMENT], U8, name="w_bytes_part", align_bytes=64)
         nc.vector.tensor_copy(
             w_bytes_part[:].rearrange("p (w t m) -> p w t m", w=2, t=PACK),
             w_bytes_raw[:].rearrange("p w (m t) -> p w t m", t=PACK),
         )
-        for q in range(4):
+        for q in range(QUADRANTS):
             nc.scalar.dma_start(w_rows[32 * q : 32 * q + 4, :].bitcast(I32), w_bytes_part[32 * q : 32 * q + 32, :].bitcast(I32))
         gs_sb = keep.tile([P, PACK], F32, name="gs_sb")
         nc.gpsimd.dma_start(gs_sb[:], gs.rearrange("(p t) o -> p (t o)", t=PACK))
@@ -74,10 +99,13 @@ def tile_picked_dhqsendhoppagex_none_p_kernel(
             tile = keep.tile([P, 2 * H], U8, name=name, align_bytes=64)
             nc.sync.dma_start(tile[:].bitcast(I32), words[0].bitcast(I32))
             w_raw.append(tile)
-        nc.gpsimd.dma_start(d_byte_table[0:P:8, :].bitcast(I32), d_scales[0].bitcast(I32))
 
-        neg_gs = keep.tile([P, PACK], F32, name="neg_gs")
-        nc.scalar.activation(neg_gs[:], gs_sb[:], COPY, scale=-1.0)
+        nc.gpsimd.dma_start(d_byte_table[0:P:BLOCK_PARTITIONS, :].bitcast(I32), d_scales[0].bitcast(I32))
+        d_word_table = keep.tile([P, G], I32, name="d_word_table", align_bytes=64)
+        nc.gpsimd.dma_start(d_word_table[:], d_words[0].rearrange("p c r -> p (c r)").bitcast(I32))
+
+        neg_gs = keep.tile([P, 1], F32, name="neg_gs")
+        nc.scalar.activation(neg_gs[:], gs_sb[:, LAST : LAST + 1], COPY, scale=-1.0)
 
         x_bytes = keep.tile([P, 2 * S], U8, name="x_bytes", tag="page0", align_bytes=64)
         nc.vector.tensor_copy(x_bytes[:, 0:S], x_byte_table[:].indirect(offs_sb[:]))
@@ -86,8 +114,8 @@ def tile_picked_dhqsendhoppagex_none_p_kernel(
 
         w_plane = keep.tile([P, 2 * H], U8, name="w_plane", tag="page2", align_bytes=64)
         nc.scalar.copy(
-            w_plane[:].bitcast(U32).rearrange("p (b e m) -> p b e m", b=2 * PACK, e=8),
-            w_rows[:].bitcast(U32).rearrange("p (e b m) -> p b e m", b=2 * PACK, e=8),
+            w_plane[:].bitcast(U32).rearrange("p (b e m) -> p b e m", b=2 * PACK, e=BLOCK_PARTITIONS),
+            w_rows[:].bitcast(U32).rearrange("p (e b m) -> p b e m", b=2 * PACK, e=BLOCK_PARTITIONS),
         )
         w_codes = []
         for i in range(2):
@@ -99,44 +127,42 @@ def tile_picked_dhqsendhoppagex_none_p_kernel(
             w_codes.append(tile)
 
         x_codes = []
-        for i, lst in enumerate((offs_sb, hz_sb)):
+        for i, list_tile in enumerate((offs_sb, hz_sb)):
             tile = keep.tile([P, S], U32, name="x_codes%d" % i, tag=("page3", "x_codes1")[i], align_bytes=64)
-            nc.vector.tensor_copy(tile[:], x_word_table[:].bitcast(U32).indirect(lst[:]))
+            nc.vector.tensor_copy(tile[:], x_word_table[:].bitcast(U32).indirect(list_tile[:]))
             x_codes.append(tile)
 
-        half = S // 2
-
-        def first_product(t, bank, a, width):
+        def first_product(t, bank, first, width):
             y_bank = psum.tile([P, width], F32, name="y_bank", tag="bank%d" % bank)
             for i in range(2):
                 nc.tensor.matmul_mx(
                     y_bank[:],
                     lhsT=w_codes[i][:, 2 * P * t : 2 * P * (t + 1)].bitcast(FP4X4),
                     lhsT_scale=w_plane[:, i * H + P * t : i * H + P * (t + 1)],
-                    rhs=x_codes[i][:, a : a + width].bitcast(FP8X4),
-                    rhs_scale=x_plane[:, i * S + a : i * S + a + width],
+                    rhs=x_codes[i][:, first : first + width].bitcast(FP8X4),
+                    rhs_scale=x_plane[:, i * S + first : i * S + first + width],
                     start=(i == 0),
                     stop=(i == 1),
                 )
             return y_bank
 
-        y_first = [first_product(0, 0, 0, half), first_product(0, PACK, half, half)]
-        y_ps = [None] + [first_product(t, t, 0, S) for t in range(1, PACK)]
+        y_halves = [first_product(0, 0, 0, HALF), first_product(0, PACK, HALF, HALF)]
+        y_banks = {t: first_product(t, t, 0, S) for t in range(1, PACK)}
 
         k1_sb = load_list(k1, "k1_sb")
         n1_sb = load_list(n1, "n1_sb")
         n2_sb = load_list(n2, "n2_sb")
         n3_sb = load_list(n3, "n3_sb")
-        d_bytes = reuse.tile([P, H], U8, name="d_bytes", offset=0, align_bytes=64)
+        d_bytes = reuse.tile([P, H], U8, name="d_bytes", offset=X_WORDS_AT, align_bytes=64)
         nc.vector.tensor_copy(d_bytes[:], d_byte_table[:].indirect(k1_sb[:]))
         d_bytes_dealt = keep.tile([P, H], U8, name="d_bytes_dealt", align_bytes=64)
         nc.vector.tensor_copy(
             d_bytes_dealt[:].rearrange("p (t m) -> p t m", t=PACK), d_bytes[:].rearrange("p (m t) -> p t m", t=PACK)
         )
         place_scale_rows(d_plane, d_bytes_dealt)
+        d_picked = reuse.tile([P, H], U32, name="d_picked", offset=X_WORDS_AT + 4 * H, align_bytes=64)
+        nc.vector.tensor_copy(d_picked[:], d_word_table[:].bitcast(U32).indirect(k1_sb[:]))
 
-        d_word_table = keep.tile([P, G], I32, name="d_word_table", tag="x_codes1", align_bytes=64)
-        nc.sync.dma_start(d_word_table[:], d_words[0].rearrange("p c r -> p (c r)").bitcast(I32))
         mem_rows = mem.rearrange("(p t) c -> t p c", t=PACK)
         out_rows = out.rearrange("(p t) c -> t p c", t=PACK)
         page = []
@@ -145,67 +171,67 @@ def tile_picked_dhqsendhoppagex_none_p_kernel(
             nc.sync.dma_start(tile[:], mem_rows[t])
             page.append(tile)
 
-        z32 = reuse.tile([P, PACK, S], F32, name="z32", offset=8 * T, align_bytes=64)
+        z32 = reuse.tile([P, PACK, S], F32, name="z32", offset=Z_AT, align_bytes=64)
         sent = []
         y_sb = []
 
-        def work_tile(width, name, tag):
-            return keep.tile([P, width], F32, name=name, tag=tag, align_bytes=64)
-
-        def larger_on_gpsimd(out_ap, low, other, key):
+        def larger_off_vector(out_ap, a, b, key):
             gap = work_tile(out_ap.shape[1], "gap", "gap" + key)
-            nc.gpsimd.tensor_tensor(gap[:], other, low, ALU.subtract)
+            nc.gpsimd.tensor_tensor(gap[:], b, a, ALU.subtract)
             rise = work_tile(out_ap.shape[1], "rise", "rise" + key)
             nc.scalar.activation(rise[:], gap[:], RELU)
-            nc.gpsimd.tensor_tensor(out_ap, low, rise[:], ALU.add)
+            nc.gpsimd.tensor_tensor(out_ap, a, rise[:], ALU.add)
 
         def fetch_and_send(t):
             y = work_tile(S, "y_sb", ("y_sb0", "fetched00", "fetched01", "fetched1")[t])
             y_sb.append(y)
             if t == 0:
                 for i in range(2):
-                    nc.scalar.copy(y[:, i * half : (i + 1) * half], y_first[i][:])
+                    nc.scalar.copy(y[:, i * HALF : (i + 1) * HALF], y_halves[i][:])
             else:
-                nc.scalar.copy(y[:], y_ps[t][:])
+                nc.scalar.copy(y[:], y_banks[t][:])
             st = work_tile(S, "st", "st%d" % t)
             ds = keep.tile([P, 2 * S], F32, name="ds%d" % t)
             sent.append(ds)
-            if t in (1, 2):
+            if 0 < t < LAST:
                 fetched = work_tile(S, "fetched", "fetched%d" % t)
-                for a in range(0, S, half):
-                    nc.scalar.activation(fetched[:, a : a + half], y[:].indirect(n1_sb[:, a // 16 : (a + half) // 16]), COPY)
-                nc.vector.tensor_tensor(st[:], y_ps[t][:], fetched[:], ALU.max)
+                for first in range(0, S, HALF):
+                    nc.scalar.activation(fetched[:, first : first + HALF], y[:].indirect(entries(n1_sb, first, HALF)), COPY)
+                nc.vector.tensor_tensor(st[:], y_banks[t][:], fetched[:], ALU.max)
             else:
                 for i in range(2):
-                    a = i * half
-                    fetched = work_tile(half, "fetched", "fetched%d%d" % (t, i))
-                    nc.scalar.activation(fetched[:], y[:].indirect(n1_sb[:, a // 16 : (a + half) // 16]), COPY)
+                    first = i * HALF
+                    fetched = work_tile(HALF, "fetched", "fetched%d%d" % (t, i))
+                    nc.scalar.activation(fetched[:], y[:].indirect(entries(n1_sb, first, HALF)), COPY)
                     if t == 0:
-                        nc.vector.tensor_tensor(st[:, a : a + half], y_first[i][:], fetched[:], ALU.max)
-                        nc.vector.tensor_copy(ds[:].indirect(n2_sb[:, a // 16 : (a + half) // 16]), st[:, a : a + half])
+                        nc.vector.tensor_tensor(st[:, first : first + HALF], y_halves[i][:], fetched[:], ALU.max)
+                        nc.vector.tensor_copy(ds[:].indirect(entries(n2_sb, first, HALF)), st[:, first : first + HALF])
                     else:
-                        larger_on_gpsimd(st[:, a : a + half], y[:, a : a + half], fetched[:], "%d%d" % (t, i))
+                        larger_off_vector(st[:, first : first + HALF], y[:, first : first + HALF], fetched[:], "%d%d" % (t, i))
             if t > 0:
                 nc.vector.tensor_copy(ds[:].indirect(n2_sb[:]), st[:])
 
         for t in range(PACK):
             fetch_and_send(t)
+
         for t, tag in enumerate(("diff0", "rise30", "rise31")):
             diff = work_tile(S, "diff", tag)
             nc.gpsimd.tensor_tensor(diff[:], sent[t][:, 0:S], y_sb[t][:], ALU.subtract)
             nc.scalar.activation(z32[:, t, :], diff[:], COPY, scale=gs_sb[:, t : t + 1])
-        last = PACK - 1
-        ngy = work_tile(S, "neg_gy", "gap30")
-        nc.scalar.activation(ngy[:], y_ps[last][:], COPY, scale=neg_gs[:, last : last + 1])
-        for a in range(0, S, CHUNK):
+        neg_gy = work_tile(S, "neg_gy", "gap30")
+        nc.scalar.activation(neg_gy[:], y_banks[LAST][:], COPY, scale=neg_gs[:])
+        for first in range(0, S, CHUNK):
             nc.vector.scalar_tensor_tensor(
-                z32[:, last, a : a + CHUNK], sent[last][:, a : a + CHUNK], gs_sb[:, last : last + 1], ngy[:, a : a + CHUNK], ALU.mult, ALU.add
+                z32[:, LAST, first : first + CHUNK],
+                sent[LAST][:, first : first + CHUNK],
+                gs_sb[:, LAST : LAST + 1],
+                neg_gy[:, first : first + CHUNK],
+                ALU.mult,
+                ALU.add,
             )
-        d_picked = keep.tile([P, H], U32, name="d_picked", tag="st3", align_bytes=64)
-        nc.vector.tensor_copy(d_picked[:], d_word_table[:].bitcast(U32).indirect(k1_sb[:]))
-        d_codes = keep.tile([P, H], U32, name="d_codes", align_bytes=64)
+        d_codes = keep.tile([P, H], U32, name="d_codes", tag="st3", align_bytes=64)
         nc.vector.tensor_copy(
-            d_codes[:].rearrange("p (t c i) -> p c t i", t=PACK, i=4), d_picked[:].rearrange("p (c i t) -> p c t i", t=PACK, i=4)
+            d_codes[:].rearrange("p (t c i) -> p c t i", t=PACK, i=LINE), d_picked[:].rearrange("p (c i t) -> p c t i", t=PACK, i=LINE)
         )
 
         held = []
@@ -220,50 +246,51 @@ def tile_picked_dhqsendhoppagex_none_p_kernel(
         z_codes = keep.tile([P, S], U32, name="z_codes", align_bytes=64)
         z_plane = keep.tile([P, S], U8, name="z_plane", align_bytes=64)
 
-        def second_product(t, bank, a, width):
+        def second_product(t, bank, first, width):
             h_bank = psum.tile([P, width], F32, name="h_bank", tag="bank%d" % bank)
             nc.tensor.matmul_mx(
                 h_bank[:],
                 lhsT=d_codes[:, P * t : P * (t + 1)].bitcast(FP8X4),
                 lhsT_scale=d_plane[:, P * t : P * (t + 1)],
-                rhs=z_codes[:, a : a + width].bitcast(FP8X4),
-                rhs_scale=z_plane[:, a : a + width],
+                rhs=z_codes[:, first : first + width].bitcast(FP8X4),
+                rhs_scale=z_plane[:, first : first + width],
                 start=True,
                 stop=True,
             )
             return h_bank
 
-        def write_back(t, h_bank, a, width, tag):
+        def write_back(t, h_bank, first, width, tag):
             nw = work_tile(width, "nw", tag)
             if t < 2:
-                nc.vector.scalar_tensor_tensor(nw[:], h_bank[:], 0.0625, held[t][:, a : a + width], ALU.mult, ALU.max)
+                nc.vector.scalar_tensor_tensor(nw[:], h_bank[:], 0.0625, held[t][:, first : first + width], ALU.mult, ALU.max)
             else:
                 h = work_tile(width, "h", "h%d" % t)
                 nc.scalar.activation(h[:], h_bank[:], COPY, scale=0.0625)
-                larger_on_gpsimd(nw[:], h[:], held[t][:], "h%d" % t)
-            nc.vector.tensor_copy(page[t][:].indirect(n3_sb[:, a // 16 : (a + width) // 16]), nw[:])
+                larger_off_vector(nw[:], h[:], held[t][:], "h%d" % t)
+            nc.vector.tensor_copy(page[t][:].indirect(entries(n3_sb, first, width)), nw[:])
 
         for c in range(S // CHUNK):
-            a = c * CHUNK
+            first = c * CHUNK
             z16 = keep.tile([P, CHUNK, PACK], BF16, name="z16_%d" % c, tag="z16_%d" % c, align_bytes=64)
             nc.scalar.copy(
-                z16[:].rearrange("p (c i) t -> p c t i", i=4), z32[:, :, a : a + CHUNK].rearrange("p t (c i) -> p c t i", i=4)
+                z16[:].rearrange("p (c i) t -> p c t i", i=LINE), z32[:, :, first : first + CHUNK].rearrange("p t (c i) -> p c t i", i=LINE)
             )
             nc.vector.quantize_mx(
-                z_codes[:, a : a + CHUNK].bitcast(FP8X4), z_plane[:, a : a + CHUNK], z16[:].rearrange("p j t -> p (j t)")
+                z_codes[:, first : first + CHUNK].bitcast(FP8X4), z_plane[:, first : first + CHUNK], z16[:].rearrange("p j t -> p (j t)")
             )
         for t in range(2, PACK):
-            fetch_held(t, reuse.tile([P, S], F32, name="held%d" % t, offset=8 * T + 4 * S * t, align_bytes=64))
-        h_first = [second_product(0, 0, 0, half)]
-        h_ps = {1: second_product(1, PACK + 1, 0, S)}
-        h_first.append(second_product(0, 1, half, half))
+            fetch_held(t, reuse.tile([P, S], F32, name="held%d" % t, offset=Z_AT + 4 * S * t, align_bytes=64))
+
+        h_early = second_product(0, 0, 0, HALF)
+        h_banks = {1: second_product(1, PACK + 1, 0, S)}
+        h_late = second_product(0, 1, HALF, HALF)
         for t in range(2, PACK):
-            h_ps[t] = second_product(t, PACK + t, 0, S)
-        write_back(0, h_first[0], 0, half, "z16_2")
-        write_back(1, h_ps[1], 0, S, "nw1")
+            h_banks[t] = second_product(t, PACK + t, 0, S)
+        write_back(0, h_early, 0, HALF, "z16_2")
+        write_back(1, h_banks[1], 0, S, "nw1")
         nc.sync.dma_start(out_rows[1], page[1][:])
-        write_back(0, h_first[1], half, half, "nw0")
+        write_back(0, h_late, HALF, HALF, "nw0")
         nc.sync.dma_start(out_rows[0], page[0][:])
         for t in range(2, PACK):
-            write_back(t, h_ps[t], 0, S, "nw%d" % t)
+            write_back(t, h_banks[t], 0, S, "nw%d" % t)
             nc.sync.dma_start(out_rows[t], page[t][:])

from contextlib import ExitStack

import concourse.mybir as mybir

K, T, S, H, G, U = 512, 1024, 512, 512, 2048, 1024
FLOPS = 2 * 3 * K * H * S

F32 = mybir.dt.float32
BF16 = mybir.dt.bfloat16
I32 = mybir.dt.int32
U32 = mybir.dt.uint32
U16 = mybir.dt.uint16
U8 = mybir.dt.uint8
FP8X4 = mybir.dt.float8_e4m3fn_x4
FP4X4 = mybir.dt.float4_e2m1fn_x4
ALU = mybir.AluOpType
COPY = mybir.ActivationFunctionType.Copy
RELU = mybir.ActivationFunctionType.Relu

P = 128
PACK = 4
LAST = PACK - 1
QUADRANTS = 4
BLOCK_PARTITIONS = 8
BLOCK_ROWS = P // BLOCK_PARTITIONS
PER_COLUMN = 16
HALF = S // 2
CHUNK = 128
LINE = 4
SEGMENT = H // BLOCK_PARTITIONS

X_WORDS_AT = 0
X_BYTES_AT = 4 * T
Z_AT = 8 * T


def tile_picked_dhqsendhoppagex_none_p_kernel(
    tc, x_words, x_scales, w1_words, w1_scales, w2_words, w2_scales, gs, d_words, d_scales, mem, offs, hz, n1, n2, k1, n3, out
):
    nc = tc.nc
    with ExitStack() as ctx:
        lists = ctx.enter_context(tc.tile_pool(name="lists", bufs=1))
        keep = ctx.enter_context(tc.tile_pool(name="keep", bufs=1))
        reuse = ctx.enter_context(tc.tile_pool(name="reuse", bufs=1))
        psum = ctx.enter_context(tc.psum_pool(name="psum", bufs=1))

        def load_list(src, name):
            tile = lists.tile([P, S // PER_COLUMN], U16, name=name)
            nc.sync.dma_start(tile[:], src)
            return tile

        def entries(list_tile, first, count):
            return list_tile[:, first // PER_COLUMN : (first + count) // PER_COLUMN]

        def zeroed_bytes(width, name, tag):
            tile = keep.tile([P, width], U8, name=name, tag=tag, align_bytes=64)
            nc.vector.memset(tile[:].bitcast(I32), 0)
            return tile

        def place_scale_rows(plane, picked):
            for q in range(QUADRANTS):
                nc.sync.dma_start(
                    plane[32 * q : 32 * q + 4, :].bitcast(I32), picked[32 * q : 32 * q + 32 : BLOCK_PARTITIONS, :].bitcast(I32)
                )

        def work_tile(width, name, tag):
            return keep.tile([P, width], F32, name=name, tag=tag, align_bytes=64)

        x_byte_table = reuse.tile([P, T], U8, name="x_byte_table", offset=X_BYTES_AT, align_bytes=64)
        w_rows = zeroed_bytes(2 * H, "w_rows", "w_rows")
        d_byte_table = zeroed_bytes(G, "d_byte_table", "d_byte_table")
        x_plane = zeroed_bytes(2 * S, "x_plane", "page1")
        d_plane = zeroed_bytes(H, "d_plane", "d_plane")

        offs_sb = load_list(offs, "offs_sb")
        nc.sync.dma_start(
            x_byte_table[:].bitcast(I32), x_scales[0].bitcast(I32).unsqueeze(1).to_broadcast([BLOCK_ROWS, BLOCK_PARTITIONS, T // 4])
        )
        hz_sb = load_list(hz, "hz_sb")
        x_word_table = reuse.tile([P, T], I32, name="x_word_table", offset=X_WORDS_AT, align_bytes=64)
        nc.sync.dma_start(x_word_table[:], x_words[0].rearrange("p c r -> p (c r)").bitcast(I32))

        w_bytes_raw = keep.tile([P, 2, SEGMENT], U8, name="w_bytes_raw", align_bytes=64)
        for i, scales in enumerate((w1_scales, w2_scales)):
            nc.scalar.dma_start(
                w_bytes_raw[:, i, :].bitcast(I32), scales[0].rearrange("r (e b) -> (r e) b", e=BLOCK_PARTITIONS).bitcast(I32)
            )
        w_bytes_part = keep.tile([P, 2 * SEGMENT], U8, name="w_bytes_part", align_bytes=64)
        nc.vector.tensor_copy(
            w_bytes_part[:].rearrange("p (w t m) -> p w t m", w=2, t=PACK),
            w_bytes_raw[:].rearrange("p w (m t) -> p w t m", t=PACK),
        )
        for q in range(QUADRANTS):
            nc.scalar.dma_start(w_rows[32 * q : 32 * q + 4, :].bitcast(I32), w_bytes_part[32 * q : 32 * q + 32, :].bitcast(I32))
        gs_sb = keep.tile([P, PACK], F32, name="gs_sb")
        nc.gpsimd.dma_start(gs_sb[:], gs.rearrange("(p t) o -> p (t o)", t=PACK))
        w_raw = []
        for name, words in (("w1_raw", w1_words), ("w2_raw", w2_words)):
            tile = keep.tile([P, 2 * H], U8, name=name, align_bytes=64)
            nc.sync.dma_start(tile[:].bitcast(I32), words[0].bitcast(I32))
            w_raw.append(tile)

        nc.gpsimd.dma_start(d_byte_table[0:P:BLOCK_PARTITIONS, :].bitcast(I32), d_scales[0].bitcast(I32))
        d_word_table = keep.tile([P, G], I32, name="d_word_table", align_bytes=64)
        nc.gpsimd.dma_start(d_word_table[:], d_words[0].rearrange("p c r -> p (c r)").bitcast(I32))

        neg_gs = keep.tile([P, 1], F32, name="neg_gs")
        nc.scalar.activation(neg_gs[:], gs_sb[:, LAST : LAST + 1], COPY, scale=-1.0)

        x_bytes = keep.tile([P, 2 * S], U8, name="x_bytes", tag="page0", align_bytes=64)
        nc.vector.tensor_copy(x_bytes[:, 0:S], x_byte_table[:].indirect(offs_sb[:]))
        nc.vector.tensor_copy(x_bytes[:, S : 2 * S], x_byte_table[:].indirect(hz_sb[:]))
        place_scale_rows(x_plane, x_bytes)

        w_plane = keep.tile([P, 2 * H], U8, name="w_plane", tag="page2", align_bytes=64)
        nc.scalar.copy(
            w_plane[:].bitcast(U32).rearrange("p (b e m) -> p b e m", b=2 * PACK, e=BLOCK_PARTITIONS),
            w_rows[:].bitcast(U32).rearrange("p (e b m) -> p b e m", b=2 * PACK, e=BLOCK_PARTITIONS),
        )
        w_codes = []
        for i in range(2):
            tile = keep.tile([P, 2 * H], U8, name="w_codes%d" % i, align_bytes=64)
            nc.scalar.copy(
                tile[:].bitcast(U16).rearrange("p (t m) -> p t m", t=PACK),
                w_raw[i][:].bitcast(U16).rearrange("p (m t) -> p t m", t=PACK),
            )
            w_codes.append(tile)

        x_codes = []
        for i, list_tile in enumerate((offs_sb, hz_sb)):
            tile = keep.tile([P, S], U32, name="x_codes%d" % i, tag=("page3", "x_codes1")[i], align_bytes=64)
            nc.vector.tensor_copy(tile[:], x_word_table[:].bitcast(U32).indirect(list_tile[:]))
            x_codes.append(tile)

        def first_product(t, bank, first, width):
            y_bank = psum.tile([P, width], F32, name="y_bank", tag="bank%d" % bank)
            for i in range(2):
                nc.tensor.matmul_mx(
                    y_bank[:],
                    lhsT=w_codes[i][:, 2 * P * t : 2 * P * (t + 1)].bitcast(FP4X4),
                    lhsT_scale=w_plane[:, i * H + P * t : i * H + P * (t + 1)],
                    rhs=x_codes[i][:, first : first + width].bitcast(FP8X4),
                    rhs_scale=x_plane[:, i * S + first : i * S + first + width],
                    start=(i == 0),
                    stop=(i == 1),
                )
            return y_bank

        y_halves = [first_product(0, 0, 0, HALF), first_product(0, PACK, HALF, HALF)]
        y_banks = {t: first_product(t, t, 0, S) for t in range(1, PACK)}

        k1_sb = load_list(k1, "k1_sb")
        n1_sb = load_list(n1, "n1_sb")
        n2_sb = load_list(n2, "n2_sb")
        n3_sb = load_list(n3, "n3_sb")
        d_bytes = reuse.tile([P, H], U8, name="d_bytes", offset=X_WORDS_AT, align_bytes=64)
        nc.vector.tensor_copy(d_bytes[:], d_byte_table[:].indirect(k1_sb[:]))
        d_bytes_dealt = keep.tile([P, H], U8, name="d_bytes_dealt", align_bytes=64)
        nc.vector.tensor_copy(
            d_bytes_dealt[:].rearrange("p (t m) -> p t m", t=PACK), d_bytes[:].rearrange("p (m t) -> p t m", t=PACK)
        )
        place_scale_rows(d_plane, d_bytes_dealt)
        d_picked = reuse.tile([P, H], U32, name="d_picked", offset=X_WORDS_AT + 4 * H, align_bytes=64)
        nc.vector.tensor_copy(d_picked[:], d_word_table[:].bitcast(U32).indirect(k1_sb[:]))

        mem_rows = mem.rearrange("(p t) c -> t p c", t=PACK)
        out_rows = out.rearrange("(p t) c -> t p c", t=PACK)
        page = []
        for t in range(PACK):
            tile = keep.tile([P, U], F32, name="page%d" % t, tag="page%d" % t, align_bytes=64)
            nc.sync.dma_start(tile[:], mem_rows[t])
            page.append(tile)

        z32 = reuse.tile([P, PACK, S], F32, name="z32", offset=Z_AT, align_bytes=64)
        sent = []
        y_sb = []

        def larger_off_vector(out_ap, a, b, key):
            gap = work_tile(out_ap.shape[1], "gap", "gap" + key)
            nc.gpsimd.tensor_tensor(gap[:], b, a, ALU.subtract)
            rise = work_tile(out_ap.shape[1], "rise", "rise" + key)
            nc.scalar.activation(rise[:], gap[:], RELU)
            nc.gpsimd.tensor_tensor(out_ap, a, rise[:], ALU.add)

        def fetch_and_send(t):
            y = work_tile(S, "y_sb", ("y_sb0", "fetched00", "fetched01", "fetched1")[t])
            y_sb.append(y)
            if t == 0:
                for i in range(2):
                    nc.scalar.copy(y[:, i * HALF : (i + 1) * HALF], y_halves[i][:])
            else:
                nc.scalar.copy(y[:], y_banks[t][:])
            st = work_tile(S, "st", "st%d" % t)
            ds = keep.tile([P, 2 * S], F32, name="ds%d" % t)
            sent.append(ds)
            if 0 < t < LAST:
                fetched = work_tile(S, "fetched", "fetched%d" % t)
                for first in range(0, S, HALF):
                    nc.scalar.activation(fetched[:, first : first + HALF], y[:].indirect(entries(n1_sb, first, HALF)), COPY)
                nc.vector.tensor_tensor(st[:], y_banks[t][:], fetched[:], ALU.max)
            else:
                for i in range(2):
                    first = i * HALF
                    fetched = work_tile(HALF, "fetched", "fetched%d%d" % (t, i))
                    nc.scalar.activation(fetched[:], y[:].indirect(entries(n1_sb, first, HALF)), COPY)
                    if t == 0:
                        nc.vector.tensor_tensor(st[:, first : first + HALF], y_halves[i][:], fetched[:], ALU.max)
                        nc.vector.tensor_copy(ds[:].indirect(entries(n2_sb, first, HALF)), st[:, first : first + HALF])
                    else:
                        larger_off_vector(st[:, first : first + HALF], y[:, first : first + HALF], fetched[:], "%d%d" % (t, i))
            if t > 0:
                nc.vector.tensor_copy(ds[:].indirect(n2_sb[:]), st[:])

        for t in range(PACK):
            fetch_and_send(t)

        for t, tag in enumerate(("diff0", "rise30", "rise31")):
            diff = work_tile(S, "diff", tag)
            nc.gpsimd.tensor_tensor(diff[:], sent[t][:, 0:S], y_sb[t][:], ALU.subtract)
            nc.scalar.activation(z32[:, t, :], diff[:], COPY, scale=gs_sb[:, t : t + 1])
        neg_gy = work_tile(S, "neg_gy", "gap30")
        nc.scalar.activation(neg_gy[:], y_banks[LAST][:], COPY, scale=neg_gs[:])
        for first in range(0, S, CHUNK):
            nc.vector.scalar_tensor_tensor(
                z32[:, LAST, first : first + CHUNK],
                sent[LAST][:, first : first + CHUNK],
                gs_sb[:, LAST : LAST + 1],
                neg_gy[:, first : first + CHUNK],
                ALU.mult,
                ALU.add,
            )
        d_codes = keep.tile([P, H], U32, name="d_codes", tag="st3", align_bytes=64)
        nc.vector.tensor_copy(
            d_codes[:].rearrange("p (t c i) -> p c t i", t=PACK, i=LINE), d_picked[:].rearrange("p (c i t) -> p c t i", t=PACK, i=LINE)
        )

        held = []

        def fetch_held(t, tile):
            nc.scalar.activation(tile[:], page[t][:].indirect(n3_sb[:]), COPY, scale=0.5)
            held.append(tile)

        fetch_held(0, work_tile(S, "held0", "gap31"))
        fetch_held(1, work_tile(S, "held1", "rise30"))

        z_codes = keep.tile([P, S], U32, name="z_codes", align_bytes=64)
        z_plane = keep.tile([P, S], U8, name="z_plane", align_bytes=64)

        def second_product(t, bank, first, width):
            h_bank = psum.tile([P, width], F32, name="h_bank", tag="bank%d" % bank)
            nc.tensor.matmul_mx(
                h_bank[:],
                lhsT=d_codes[:, P * t : P * (t + 1)].bitcast(FP8X4),
                lhsT_scale=d_plane[:, P * t : P * (t + 1)],
                rhs=z_codes[:, first : first + width].bitcast(FP8X4),
                rhs_scale=z_plane[:, first : first + width],
                start=True,
                stop=True,
            )
            return h_bank

        def write_back(t, h_bank, first, width, tag):
            nw = work_tile(width, "nw", tag)
            if t < 2:
                nc.vector.scalar_tensor_tensor(nw[:], h_bank[:], 0.0625, held[t][:, first : first + width], ALU.mult, ALU.max)
            else:
                h = work_tile(width, "h", "h%d" % t)
                nc.scalar.activation(h[:], h_bank[:], COPY, scale=0.0625)
                larger_off_vector(nw[:], h[:], held[t][:], "h%d" % t)
            nc.vector.tensor_copy(page[t][:].indirect(entries(n3_sb, first, width)), nw[:])

        for c in range(S // CHUNK):
            first = c * CHUNK
            z16 = keep.tile([P, CHUNK, PACK], BF16, name="z16_%d" % c, tag="z16_%d" % c, align_bytes=64)
            nc.scalar.copy(
                z16[:].rearrange("p (c i) t -> p c t i", i=LINE), z32[:, :, first : first + CHUNK].rearrange("p t (c i) -> p c t i", i=LINE)
            )
            nc.vector.quantize_mx(
                z_codes[:, first : first + CHUNK].bitcast(FP8X4), z_plane[:, first : first + CHUNK], z16[:].rearrange("p j t -> p (j t)")
            )
        for t in range(2, PACK):
            fetch_held(t, reuse.tile([P, S], F32, name="held%d" % t, offset=Z_AT + 4 * S * t, align_bytes=64))

        h_early = second_product(0, 0, 0, HALF)
        h_banks = {1: second_product(1, PACK + 1, 0, S)}
        h_late = second_product(0, 1, HALF, HALF)
        for t in range(2, PACK):
            h_banks[t] = second_product(t, PACK + t, 0, S)
        write_back(0, h_early, 0, HALF, "z16_2")
        write_back(1, h_banks[1], 0, S, "nw1")
        nc.sync.dma_start(out_rows[1], page[1][:])
        write_back(0, h_late, HALF, HALF, "nw0")
        nc.sync.dma_start(out_rows[0], page[0][:])
        for t in range(2, PACK):
            write_back(t, h_banks[t], 0, S, "nw%d" % t)
            nc.sync.dma_start(out_rows[t], page[t][:])
